import numpy as np
import ml_dtypes


def mxq(x, axis, fmt="e4m3"):
    dtype, down = {"e4m3": (ml_dtypes.float8_e4m3fn, 7), "e5m2": (ml_dtypes.float8_e5m2, 14)}[fmt]
    v = np.moveaxis(np.asarray(x, np.float32).astype(ml_dtypes.bfloat16).astype(np.float64), axis, -1)
    blocks = v.reshape(v.shape[:-1] + (-1, 32))
    amax = np.abs(blocks).max(-1, keepdims=True)
    byte = np.maximum(np.where(amax > 0, np.frexp(amax)[1] - 1 + 127, 0) - down, 1)
    scale = np.exp2(byte - 127.0)
    codes = (blocks / scale).astype(np.float32).astype(dtype).astype(np.float64)
    return np.moveaxis((codes * scale).reshape(v.shape), -1, axis)


WIDE = False


def mx_kscale(k):
    if not WIDE:
        return np.ones(k)
    levels = np.array([10, -10, 5, -5, 0])
    if k % 512:
        return np.exp2(np.random.permutation(np.resize(levels, k // 32))).repeat(32)
    a = np.empty((k // 512, 16))
    for p in range(k // 512):
        a[p, :8] = np.random.permutation(np.resize(levels, 8))
        for g in range(8):
            far = levels[np.abs(levels - a[p, g]) >= 10]
            a[p, g + 8] = far[np.random.randint(len(far))]
    return np.exp2(a.ravel()).repeat(32)


def f64(x):
    return np.asarray(x).astype(np.float64)


E2M1 = np.array([0.0, 0.5, 1.0, 1.5, 2.0, 3.0, 4.0, 6.0, -0.0, -0.5, -1.0, -1.5, -2.0, -3.0, -4.0, -6.0])


def pack_weight(w, fmt):
    k, n = w.shape
    w = f64(np.asarray(w, np.float32).astype(ml_dtypes.bfloat16)).reshape(k // 32, 32, n)
    amax = np.abs(w).max(1)
    if fmt == "e4m3":
        byte = np.frexp(amax)[1] - 1 + 127 - 7
    else:
        mant, ex = np.frexp(amax / 6.0)
        byte = np.where(mant > 0.5, ex, ex - 1) + 127
    byte = np.clip(np.where(amax > 0, byte, 1), 1, 254)
    scaled = (w * np.exp2(127.0 - byte)[:, None, :]).reshape(k, n).astype(np.float32)
    by_word = np.ascontiguousarray(scaled.reshape(k // 512, 128, 4, n).transpose(0, 1, 3, 2))
    if fmt == "e4m3":
        words = by_word.astype(ml_dtypes.float8_e4m3fn).view(np.uint8)
    else:
        c = by_word.astype(ml_dtypes.float4_e2m1fn).view(np.uint8) & 0xF
        words = (c[..., 0::2] | (c[..., 1::2] << 4)).reshape(k // 512, 128, 2 * n)
    return np.ascontiguousarray(words), np.ascontiguousarray(byte.astype(np.uint8).reshape(k // 512, 16, n))


def unpack_weight(words, scales, fmt):
    g, _, n = scales.shape
    words = np.ascontiguousarray(words).reshape(g, 128, n, -1)
    if fmt == "e4m3":
        vals = words.view(ml_dtypes.float8_e4m3fn).astype(np.float64)
    else:
        nib = np.empty((g, 128, n, 4), np.uint8)
        nib[..., 0::2] = words & 0xF
        nib[..., 1::2] = words >> 4
        vals = E2M1[nib]
    vals = vals * np.repeat(np.exp2(scales.astype(np.float64) - 127.0), 8, axis=1)[..., None]
    return vals.transpose(0, 1, 3, 2).reshape(g * 512, n)


K, M, T = 2048, 1024, 512


def setup_inputs():
    n = np.random.standard_normal
    s = mx_kscale(K)[:, None]
    x = n((K, T)) * s
    x4 = pack_weight(x, "e2m1")
    rest = x - unpack_weight(*x4, "e2m1")
    p_w4 = pack_weight(n((K, M)) / np.sqrt(K) / s, "e2m1")
    return {
        "x4_words": x4[0],
        "x4_scales": x4[1],
        "xr": (rest).astype(np.float32),
        "w4_words": p_w4[0],
        "w4_scales": p_w4[1],
        "g": (n((512, 1024))).astype(np.float32),
    }


def reference(x4_words, x4_scales, xr, w4_words, w4_scales, g):
    x4_ = unpack_weight(x4_words, x4_scales, "e2m1")
    xr_ = mxq(f64(xr), 0, "e4m3")
    w4_ = unpack_weight(w4_words, w4_scales, "e2m1")
    y = x4_.T @ w4_ + xr_.T @ w4_
    return f64(g) * y

@@ -1,0 +1,152 @@
+from contextlib import ExitStack
+
+import concourse.mybir as mybir
+
+K, N, T = 2048, 1024, 512
+FLOPS = 2 * 2 * K * N * T
+
+F32 = mybir.dt.float32
+BF16 = mybir.dt.bfloat16
+U32 = mybir.dt.uint32
+I32 = mybir.dt.int32
+U8 = mybir.dt.uint8
+FP8X4 = mybir.dt.float8_e4m3fn_x4
+FP4X4 = mybir.dt.float4_e2m1fn_x4
+
+P = 128
+A = K // 512
+TT = T // P
+NH = 2
+HALF = N // NH
+VCOLS = 384
+
+
+def tile_mix_xres_tm_mul_kernel(tc, x4_words, x4_scales, xr, w4_words, w4_scales, g, out):
+    nc = tc.nc
+    with ExitStack() as ctx:
+        keep = ctx.enter_context(tc.tile_pool(name="keep", bufs=1))
+        psum = ctx.enter_context(tc.psum_pool(name="psum", bufs=1))
+        ctx.enter_context(tc.manual_schedule())
+
+        x0 = keep.tile([P, 1, 2 * T], U8, name="x0", align_bytes=256)
+        x123 = keep.tile([P, A - 1, 2 * T], U8, name="x123", align_bytes=256)
+        w0 = keep.tile([P, 1, 2 * N], U8, name="w0", align_bytes=256)
+        w123 = keep.tile([P, A - 1, 2 * N], U8, name="w123", align_bytes=256)
+        xs = keep.tile([P, A, T], U8, name="xs", align_bytes=256)
+        ws0 = keep.tile([P, 1, N], U8, name="ws0", align_bytes=256)
+        ws123 = keep.tile([P, A - 1, N], U8, name="ws123", align_bytes=256)
+        dummy = keep.tile([P, 8], F32, name="dummy")
+        dummy_out = keep.tile([P, 8], F32, name="dummy_out")
+
+        def flat_i32(t):
+            return t[:].rearrange("p a n -> p (a n)").bitcast(I32)
+
+        nc.vector.memset(flat_i32(xs), 0)
+        nc.vector.memset(flat_i32(ws0), 0)
+        nc.vector.memset(flat_i32(ws123), 0)
+        nc.vector.memset(dummy[:], 0.0)
+
+        def load_scales(engine, tile, dram, a0, a1, r):
+            n4 = dram.shape[2] // 4
+            engine.dma_start(
+                out=flat_i32(tile)[r:P:32, :].rearrange("q (a n) -> q a n", n=n4),
+                in_=dram.bitcast(I32)[a0:a1, r:16:4, :].rearrange("a q n -> q a n"),
+            )
+
+        nc.sync.dma_start(out=x0[:, 0, :], in_=x4_words[0])
+        nc.sync.dma_start(out=w0[:, 0, :], in_=w4_words[0])
+        for r in range(4):
+            load_scales(nc.scalar, xs, x4_scales, 0, A, r)
+        for r in range(4):
+            load_scales(nc.sync, ws0, w4_scales, 0, 1, r)
+        for r in range(4):
+            load_scales(nc.sync, ws123, w4_scales, 1, A, r)
+        nc.sync.dma_start(out=w123[:], in_=w4_words[1:A].rearrange("a p n -> p a n"))
+        nc.sync.dma_start(out=x123[:], in_=x4_words[1:A].rearrange("a p n -> p a n"))
+        nc.scalar.copy(dummy_out[:], dummy[:])
+
+        raw = []
+        for a in range(A):
+            raw_a = keep.tile([P, 4, T], F32, name="raw%d" % a, align_bytes=256)
+            nc.sync.dma_start(out=raw_a[:], in_=xr[512 * a : 512 * (a + 1), :].rearrange("(p j) t -> p j t", j=4))
+            raw.append(raw_a)
+        g_sb = []
+        for t in range(TT):
+            g_t = keep.tile([P, N], F32, name="g%d" % t, align_bytes=256)
+            nc.sync.dma_start(out=g_t[:], in_=g[P * t : P * (t + 1), :])
+            g_sb.append(g_t)
+
+        banks = []
+        for i in range(TT * NH):
+            bank = psum.tile([P, HALF], F32, name="bank%d" % i)
+            banks.append(bank)
+
+        def w_operand(a, h):
+            words, scales, b = (w0, ws0, 0) if a == 0 else (w123, ws123, a - 1)
+            return (
+                words[:, b, 2 * HALF * h : 2 * HALF * (h + 1)].bitcast(FP4X4),
+                scales[:, b, HALF * h : HALF * (h + 1)],
+            )
+
+        def x4_pass(a, t, h):
+            words, b = (x0, 0) if a == 0 else (x123, a - 1)
+            rhs, rhs_scale = w_operand(a, h)
+            nc.tensor.matmul_mx(
+                out=banks[NH * t + h][:],
+                lhsT=words[:, b, 2 * P * t : 2 * P * (t + 1)].bitcast(FP4X4),
+                lhsT_scale=xs[:, a, P * t : P * (t + 1)],
+                rhs=rhs,
+                rhs_scale=rhs_scale,
+                start=(a == 0),
+                stop=False,
+            )
+
+        for a in range(A):
+            for h in range(NH):
+                for t in range(TT):
+                    x4_pass(a, t, h)
+
+        codes, scales = [], []
+        for a in range(A):
+            xb = keep.tile([P, T, 4], BF16, name="xb%d" % a, align_bytes=256)
+            c_a = keep.tile([P, T], U32, name="codes%d" % a, align_bytes=256)
+            s_a = keep.tile([P, T], U8, name="scales%d" % a, align_bytes=256)
+            nc.vector.tensor_copy(out=xb[:, 0:VCOLS, :], in_=raw[a][:, :, 0:VCOLS].rearrange("p j t -> p t j"))
+            nc.scalar.copy(xb[:, VCOLS:T, :], raw[a][:, :, VCOLS:T].rearrange("p j t -> p t j"))
+            nc.vector.quantize_mx(
+                out=c_a[:].bitcast(FP8X4), scales=s_a[:], in_=xb[:].rearrange("p t j -> p (t j)")
+            )
+            codes.append(c_a)
+            scales.append(s_a)
+
+        def xr_pass(a, t, h):
+            rhs, rhs_scale = w_operand(a, h)
+            nc.tensor.matmul_mx(
+                out=banks[NH * t + h][:],
+                lhsT=codes[a][:, P * t : P * (t + 1)].bitcast(FP8X4),
+                lhsT_scale=scales[a][:, P * t : P * (t + 1)],
+                rhs=rhs,
+                rhs_scale=rhs_scale,
+                start=False,
+                stop=(a == A - 1),
+            )
+
+        for t in range(TT):
+            for h in range(NH):
+                xr_pass(0, t, h)
+
+        for t in range(TT):
+            for h in range(NH):
+                i = NH * t + h
+                for a in range(1, A):
+                    xr_pass(a, t, h)
+                result = keep.tile([P, HALF], F32, name="result%d" % i, align_bytes=256)
+                parts = 2 if i == TT * NH - 1 else 1
+                width = HALF // parts
+                for j in range(parts):
+                    cols = slice(width * j, width * (j + 1))
+                    n_cols = slice(HALF * h + width * j, HALF * h + width * (j + 1))
+                    nc.vector.tensor_tensor(
+                        out=result[:, cols], in0=banks[i][:, cols], in1=g_sb[t][:, n_cols], op=mybir.AluOpType.mult
+                    )
+                    nc.sync.dma_start(out=out[P * t : P * (t + 1), n_cols], in_=result[:, cols])

@@ -31,10 +31,10 @@ def tile_mix_xres_tm_mul_kernel(tc, x4_words, x4_scales, xr, w4_words, w4_scales
         x0 = keep.tile([P, 1, 2 * T], U8, name="x0", align_bytes=256)
         x123 = keep.tile([P, A - 1, 2 * T], U8, name="x123", align_bytes=256)
         w0 = keep.tile([P, 1, 2 * N], U8, name="w0", align_bytes=256)
-        w123 = keep.tile([P, A - 1, 2 * N], U8, name="w123", align_bytes=256)
+        w1 = keep.tile([P, 1, 2 * N], U8, name="w1", align_bytes=256)
+        w23 = keep.tile([P, 2, 2 * N], U8, name="w23", align_bytes=256)
         xs = keep.tile([P, A, T], U8, name="xs", align_bytes=256)
-        ws0 = keep.tile([P, 1, N], U8, name="ws0", align_bytes=256)
-        ws123 = keep.tile([P, A - 1, N], U8, name="ws123", align_bytes=256)
+        ws = keep.tile([P, A, N], U8, name="ws", align_bytes=256)
         dummy = keep.tile([P, 8], F32, name="dummy")
         dummy_out = keep.tile([P, 8], F32, name="dummy_out")
 
@@ -42,34 +42,36 @@ def tile_mix_xres_tm_mul_kernel(tc, x4_words, x4_scales, xr, w4_words, w4_scales
             return t[:].rearrange("p a n -> p (a n)").bitcast(I32)
 
         nc.vector.memset(flat_i32(xs), 0)
-        nc.vector.memset(flat_i32(ws0), 0)
-        nc.vector.memset(flat_i32(ws123), 0)
+        nc.vector.memset(flat_i32(ws), 0)
         nc.vector.memset(dummy[:], 0.0)
 
-        def load_scales(engine, tile, dram, a0, a1, r):
+        def load_scales(engine, tile, dram, r):
             n4 = dram.shape[2] // 4
             engine.dma_start(
                 out=flat_i32(tile)[r:P:32, :].rearrange("q (a n) -> q a n", n=n4),
-                in_=dram.bitcast(I32)[a0:a1, r:16:4, :].rearrange("a q n -> q a n"),
+                in_=dram.bitcast(I32)[:, r:16:4, :].rearrange("a q n -> q a n"),
             )
-
-        nc.sync.dma_start(out=x0[:, 0, :], in_=x4_words[0])
-        nc.sync.dma_start(out=w0[:, 0, :], in_=w4_words[0])
-        for r in range(4):
-            load_scales(nc.scalar, xs, x4_scales, 0, A, r)
-        for r in range(4):
-            load_scales(nc.sync, ws0, w4_scales, 0, 1, r)
-        for r in range(4):
-            load_scales(nc.sync, ws123, w4_scales, 1, A, r)
-        nc.sync.dma_start(out=w123[:], in_=w4_words[1:A].rearrange("a p n -> p a n"))
-        nc.sync.dma_start(out=x123[:], in_=x4_words[1:A].rearrange("a p n -> p a n"))
-        nc.scalar.copy(dummy_out[:], dummy[:])
 
         raw = []
         for a in range(A):
             raw_a = keep.tile([P, 4, T], F32, name="raw%d" % a, align_bytes=256)
-            nc.sync.dma_start(out=raw_a[:], in_=xr[512 * a : 512 * (a + 1), :].rearrange("(p j) t -> p j t", j=4))
             raw.append(raw_a)
+
+        def load_raw(engine, a):
+            engine.dma_start(out=raw[a][:], in_=xr[512 * a : 512 * (a + 1), :].rearrange("(p j) t -> p j t", j=4))
+
+        nc.gpsimd.dma_start(out=x0[:, 0, :].bitcast(I32), in_=x4_words[0].bitcast(I32))
+        load_raw(nc.gpsimd, 0)
+        nc.sync.dma_start(out=w0[:, 0, :], in_=w4_words[0])
+        for r in range(4):
+            load_scales(nc.scalar, xs, x4_scales, r)
+            load_scales(nc.sync, ws, w4_scales, r)
+        nc.sync.dma_start(out=w1[:, 0, :], in_=w4_words[1])
+        nc.sync.dma_start(out=x123[:], in_=x4_words[1:A].rearrange("a p n -> p a n"))
+        nc.sync.dma_start(out=w23[:], in_=w4_words[2:A].rearrange("a p n -> p a n"))
+        nc.scalar.copy(dummy_out[:], dummy[:])
+        for a in range(1, A):
+            load_raw(nc.sync, a)
         g_sb = []
         for t in range(TT):
             g_t = keep.tile([P, N], F32, name="g%d" % t, align_bytes=256)
@@ -82,10 +84,10 @@ def tile_mix_xres_tm_mul_kernel(tc, x4_words, x4_scales, xr, w4_words, w4_scales
             banks.append(bank)
 
         def w_operand(a, h):
-            words, scales, b = (w0, ws0, 0) if a == 0 else (w123, ws123, a - 1)
+            words, b = ((w0, 0), (w1, 0), (w23, 0), (w23, 1))[a]
             return (
                 words[:, b, 2 * HALF * h : 2 * HALF * (h + 1)].bitcast(FP4X4),
-                scales[:, b, HALF * h : HALF * (h + 1)],
+                ws[:, a, HALF * h : HALF * (h + 1)],
             )
 
         def x4_pass(a, t, h):
@@ -136,17 +138,16 @@ def tile_mix_xres_tm_mul_kernel(tc, x4_words, x4_scales, xr, w4_words, w4_scales
                 xr_pass(0, t, h)
 
         for t in range(TT):
+            result = keep.tile([P, N], F32, name="result%d" % t, align_bytes=256)
+            rows = slice(P * t, P * (t + 1))
             for h in range(NH):
-                i = NH * t + h
                 for a in range(1, A):
                     xr_pass(a, t, h)
-                result = keep.tile([P, HALF], F32, name="result%d" % i, align_bytes=256)
-                parts = 2 if i == TT * NH - 1 else 1
-                width = HALF // parts
-                for j in range(parts):
-                    cols = slice(width * j, width * (j + 1))
-                    n_cols = slice(HALF * h + width * j, HALF * h + width * (j + 1))
-                    nc.vector.tensor_tensor(
-                        out=result[:, cols], in0=banks[i][:, cols], in1=g_sb[t][:, n_cols], op=mybir.AluOpType.mult
-                    )
-                    nc.sync.dma_start(out=out[P * t : P * (t + 1), n_cols], in_=result[:, cols])
+                cols = slice(HALF * h, HALF * (h + 1))
+                nc.vector.tensor_tensor(
+                    out=result[:, cols], in0=banks[NH * t + h][:], in1=g_sb[t][:, cols], op=mybir.AluOpType.mult
+                )
+                if t == TT - 1:
+                    nc.sync.dma_start(out=out[rows, cols], in_=result[:, cols])
+            if t < TT - 1:
+                nc.sync.dma_start(out=out[rows, :], in_=result[:])

@@ -18,7 +18,8 @@ A = K // 512
 TT = T // P
 NH = 2
 HALF = N // NH
-VCOLS = 384
+VCOLS = 256
+EARLY = 2
 
 
 def tile_mix_xres_tm_mul_kernel(tc, x4_words, x4_scales, xr, w4_words, w4_scales, g, out):
@@ -30,26 +31,27 @@ def tile_mix_xres_tm_mul_kernel(tc, x4_words, x4_scales, xr, w4_words, w4_scales
 
         x0 = keep.tile([P, 1, 2 * T], U8, name="x0", align_bytes=256)
         x123 = keep.tile([P, A - 1, 2 * T], U8, name="x123", align_bytes=256)
-        w0 = keep.tile([P, 1, 2 * N], U8, name="w0", align_bytes=256)
-        w1 = keep.tile([P, 1, 2 * N], U8, name="w1", align_bytes=256)
+        w01 = keep.tile([P, 2, 2 * N], U8, name="w01", align_bytes=256)
         w23 = keep.tile([P, 2, 2 * N], U8, name="w23", align_bytes=256)
         xs = keep.tile([P, A, T], U8, name="xs", align_bytes=256)
-        ws = keep.tile([P, A, N], U8, name="ws", align_bytes=256)
+        ws0 = keep.tile([P, 1, N], U8, name="ws0", align_bytes=256)
+        ws123 = keep.tile([P, A - 1, N], U8, name="ws123", align_bytes=256)
         dummy = keep.tile([P, 8], F32, name="dummy")
         dummy_out = keep.tile([P, 8], F32, name="dummy_out")
 
         def flat_i32(t):
             return t[:].rearrange("p a n -> p (a n)").bitcast(I32)
 
+        nc.vector.memset(flat_i32(ws0), 0)
         nc.vector.memset(flat_i32(xs), 0)
-        nc.vector.memset(flat_i32(ws), 0)
+        nc.vector.memset(flat_i32(ws123), 0)
         nc.vector.memset(dummy[:], 0.0)
 
-        def load_scales(engine, tile, dram, r):
+        def load_scales(engine, tile, dram, a0, a1, r):
             n4 = dram.shape[2] // 4
             engine.dma_start(
                 out=flat_i32(tile)[r:P:32, :].rearrange("q (a n) -> q a n", n=n4),
-                in_=dram.bitcast(I32)[:, r:16:4, :].rearrange("a q n -> q a n"),
+                in_=dram.bitcast(I32)[a0:a1, r:16:4, :].rearrange("a q n -> q a n"),
             )
 
         raw = []
@@ -61,16 +63,18 @@ def tile_mix_xres_tm_mul_kernel(tc, x4_words, x4_scales, xr, w4_words, w4_scales
             engine.dma_start(out=raw[a][:], in_=xr[512 * a : 512 * (a + 1), :].rearrange("(p j) t -> p j t", j=4))
 
         nc.gpsimd.dma_start(out=x0[:, 0, :].bitcast(I32), in_=x4_words[0].bitcast(I32))
-        load_raw(nc.gpsimd, 0)
-        nc.sync.dma_start(out=w0[:, 0, :], in_=w4_words[0])
-        for r in range(4):
-            load_scales(nc.scalar, xs, x4_scales, r)
-            load_scales(nc.sync, ws, w4_scales, r)
-        nc.sync.dma_start(out=w1[:, 0, :], in_=w4_words[1])
+        load_scales(nc.gpsimd, ws0, w4_scales, 0, 1, 3)
+        for r in range(3):
+            load_scales(nc.sync, ws0, w4_scales, 0, 1, r)
+            load_scales(nc.scalar, xs, x4_scales, 0, A, r)
+        load_scales(nc.scalar, xs, x4_scales, 0, A, 3)
+        nc.sync.dma_start(out=w01[:], in_=w4_words[0:2].rearrange("a p n -> p a n"))
         nc.sync.dma_start(out=x123[:], in_=x4_words[1:A].rearrange("a p n -> p a n"))
+        for r in range(4):
+            load_scales(nc.scalar, ws123, w4_scales, 1, A, r)
         nc.sync.dma_start(out=w23[:], in_=w4_words[2:A].rearrange("a p n -> p a n"))
         nc.scalar.copy(dummy_out[:], dummy[:])
-        for a in range(1, A):
+        for a in range(A):
             load_raw(nc.sync, a)
         g_sb = []
         for t in range(TT):
@@ -84,10 +88,11 @@ def tile_mix_xres_tm_mul_kernel(tc, x4_words, x4_scales, xr, w4_words, w4_scales
             banks.append(bank)
 
         def w_operand(a, h):
-            words, b = ((w0, 0), (w1, 0), (w23, 0), (w23, 1))[a]
+            scales, b_s = (ws0, 0) if a == 0 else (ws123, a - 1)
+            words, b = ((w01, 0), (w01, 1), (w23, 0), (w23, 1))[a]
             return (
                 words[:, b, 2 * HALF * h : 2 * HALF * (h + 1)].bitcast(FP4X4),
-                ws[:, a, HALF * h : HALF * (h + 1)],
+                scales[:, b_s, HALF * h : HALF * (h + 1)],
             )
 
         def x4_pass(a, t, h):
@@ -115,9 +120,12 @@ def tile_mix_xres_tm_mul_kernel(tc, x4_words, x4_scales, xr, w4_words, w4_scales
             s_a = keep.tile([P, T], U8, name="scales%d" % a, align_bytes=256)
             nc.vector.tensor_copy(out=xb[:, 0:VCOLS, :], in_=raw[a][:, :, 0:VCOLS].rearrange("p j t -> p t j"))
             nc.scalar.copy(xb[:, VCOLS:T, :], raw[a][:, :, VCOLS:T].rearrange("p j t -> p t j"))
-            nc.vector.quantize_mx(
-                out=c_a[:].bitcast(FP8X4), scales=s_a[:], in_=xb[:].rearrange("p t j -> p (t j)")
-            )
+            for t0, t1 in ((0, VCOLS), (VCOLS, T)):
+                nc.vector.quantize_mx(
+                    out=c_a[:, t0:t1].bitcast(FP8X4),
+                    scales=s_a[:, t0:t1],
+                    in_=xb[:, t0:t1, :].rearrange("p t j -> p (t j)"),
+                )
             codes.append(c_a)
             scales.append(s_a)
 
@@ -133,15 +141,16 @@ def tile_mix_xres_tm_mul_kernel(tc, x4_words, x4_scales, xr, w4_words, w4_scales
                 stop=(a == A - 1),
             )
 
-        for t in range(TT):
-            for h in range(NH):
-                xr_pass(0, t, h)
+        for a, tiles in ((0, TT), (1, EARLY)):
+            for t in range(tiles):
+                for h in range(NH):
+                    xr_pass(a, t, h)
 
         for t in range(TT):
             result = keep.tile([P, N], F32, name="result%d" % t, align_bytes=256)
             rows = slice(P * t, P * (t + 1))
             for h in range(NH):
-                for a in range(1, A):
+                for a in range(2 if t < EARLY else 1, A):
                     xr_pass(a, t, h)
                 cols = slice(HALF * h, HALF * (h + 1))
                 nc.vector.tensor_tensor(

@@ -19,6 +19,7 @@ TT = T // P
 NH = 2
 HALF = N // NH
 VCOLS = 256
+FIRST = 2
 EARLY = 2
 
 
@@ -31,51 +32,57 @@ def tile_mix_xres_tm_mul_kernel(tc, x4_words, x4_scales, xr, w4_words, w4_scales
 
         x0 = keep.tile([P, 1, 2 * T], U8, name="x0", align_bytes=256)
         x123 = keep.tile([P, A - 1, 2 * T], U8, name="x123", align_bytes=256)
-        w01 = keep.tile([P, 2, 2 * N], U8, name="w01", align_bytes=256)
+        w0 = keep.tile([P, 1, 2 * N], U8, name="w0", align_bytes=256)
+        w1 = keep.tile([P, 1, 2 * N], U8, name="w1", align_bytes=256)
         w23 = keep.tile([P, 2, 2 * N], U8, name="w23", align_bytes=256)
         xs = keep.tile([P, A, T], U8, name="xs", align_bytes=256)
-        ws0 = keep.tile([P, 1, N], U8, name="ws0", align_bytes=256)
-        ws123 = keep.tile([P, A - 1, N], U8, name="ws123", align_bytes=256)
+        ws = keep.tile([P, A, N], U8, name="ws", align_bytes=256)
         dummy = keep.tile([P, 8], F32, name="dummy")
         dummy_out = keep.tile([P, 8], F32, name="dummy_out")
 
         def flat_i32(t):
             return t[:].rearrange("p a n -> p (a n)").bitcast(I32)
 
-        nc.vector.memset(flat_i32(ws0), 0)
+        nc.vector.memset(flat_i32(ws), 0)
         nc.vector.memset(flat_i32(xs), 0)
-        nc.vector.memset(flat_i32(ws123), 0)
         nc.vector.memset(dummy[:], 0.0)
 
-        def load_scales(engine, tile, dram, a0, a1, r):
+        def load_scales(engine, tile, dram, r):
             n4 = dram.shape[2] // 4
             engine.dma_start(
                 out=flat_i32(tile)[r:P:32, :].rearrange("q (a n) -> q a n", n=n4),
-                in_=dram.bitcast(I32)[a0:a1, r:16:4, :].rearrange("a q n -> q a n"),
+                in_=dram.bitcast(I32)[:, r:16:4, :].rearrange("a q n -> q a n"),
             )
 
         raw = []
-        for a in range(A):
-            raw_a = keep.tile([P, 4, T], F32, name="raw%d" % a, align_bytes=256)
-            raw.append(raw_a)
+        for a, widths in enumerate(((VCOLS, T - VCOLS), (T,), (T,), (T,))):
+            pieces, t0 = [], 0
+            for width in widths:
+                piece = keep.tile([P, 4, width], F32, name="raw%d_%d" % (a, t0), align_bytes=256)
+                pieces.append((t0, t0 + width, piece))
+                t0 += width
+            raw.append(pieces)
 
-        def load_raw(engine, a):
-            engine.dma_start(out=raw[a][:], in_=xr[512 * a : 512 * (a + 1), :].rearrange("(p j) t -> p j t", j=4))
+        def load_raw(a, i):
+            t0, t1, piece = raw[a][i]
+            nc.sync.dma_start(
+                out=piece[:], in_=xr[512 * a : 512 * (a + 1), t0:t1].rearrange("(p j) t -> p j t", j=4)
+            )
 
-        nc.gpsimd.dma_start(out=x0[:, 0, :].bitcast(I32), in_=x4_words[0].bitcast(I32))
-        load_scales(nc.gpsimd, ws0, w4_scales, 0, 1, 3)
-        for r in range(3):
-            load_scales(nc.sync, ws0, w4_scales, 0, 1, r)
-            load_scales(nc.scalar, xs, x4_scales, 0, A, r)
-        load_scales(nc.scalar, xs, x4_scales, 0, A, 3)
-        nc.sync.dma_start(out=w01[:], in_=w4_words[0:2].rearrange("a p n -> p a n"))
-        nc.sync.dma_start(out=x123[:], in_=x4_words[1:A].rearrange("a p n -> p a n"))
+        load_raw(0, 0)
+        nc.sync.dma_start(out=w0[:, 0, :], in_=w4_words[0])
         for r in range(4):
-            load_scales(nc.scalar, ws123, w4_scales, 1, A, r)
+            load_scales(nc.sync, ws, w4_scales, r)
+        nc.sync.dma_start(out=x0[:, 0, :], in_=x4_words[0])
+        for r in range(4):
+            load_scales(nc.sync, xs, x4_scales, r)
+        nc.sync.dma_start(out=w1[:, 0, :], in_=w4_words[1])
+        nc.sync.dma_start(out=x123[:], in_=x4_words[1:A].rearrange("a p n -> p a n"))
         nc.sync.dma_start(out=w23[:], in_=w4_words[2:A].rearrange("a p n -> p a n"))
         nc.scalar.copy(dummy_out[:], dummy[:])
-        for a in range(A):
-            load_raw(nc.sync, a)
+        load_raw(0, 1)
+        for a in range(1, A):
+            load_raw(a, 0)
         g_sb = []
         for t in range(TT):
             g_t = keep.tile([P, N], F32, name="g%d" % t, align_bytes=256)
@@ -88,11 +95,10 @@ def tile_mix_xres_tm_mul_kernel(tc, x4_words, x4_scales, xr, w4_words, w4_scales
             banks.append(bank)
 
         def w_operand(a, h):
-            scales, b_s = (ws0, 0) if a == 0 else (ws123, a - 1)
-            words, b = ((w01, 0), (w01, 1), (w23, 0), (w23, 1))[a]
+            words, b = ((w0, 0), (w1, 0), (w23, 0), (w23, 1))[a]
             return (
                 words[:, b, 2 * HALF * h : 2 * HALF * (h + 1)].bitcast(FP4X4),
-                scales[:, b_s, HALF * h : HALF * (h + 1)],
+                ws[:, a, HALF * h : HALF * (h + 1)],
             )
 
         def x4_pass(a, t, h):
@@ -104,30 +110,30 @@ def tile_mix_xres_tm_mul_kernel(tc, x4_words, x4_scales, xr, w4_words, w4_scales
                 lhsT_scale=xs[:, a, P * t : P * (t + 1)],
                 rhs=rhs,
                 rhs_scale=rhs_scale,
-                start=(a == 0),
+                start=(a == 0 and t >= FIRST),
                 stop=False,
             )
 
+        xb, codes, scales = [], [], []
         for a in range(A):
-            for h in range(NH):
-                for t in range(TT):
-                    x4_pass(a, t, h)
-
-        codes, scales = [], []
-        for a in range(A):
-            xb = keep.tile([P, T, 4], BF16, name="xb%d" % a, align_bytes=256)
+            xb_a = keep.tile([P, T, 4], BF16, name="xb%d" % a, align_bytes=256)
             c_a = keep.tile([P, T], U32, name="codes%d" % a, align_bytes=256)
             s_a = keep.tile([P, T], U8, name="scales%d" % a, align_bytes=256)
-            nc.vector.tensor_copy(out=xb[:, 0:VCOLS, :], in_=raw[a][:, :, 0:VCOLS].rearrange("p j t -> p t j"))
-            nc.scalar.copy(xb[:, VCOLS:T, :], raw[a][:, :, VCOLS:T].rearrange("p j t -> p t j"))
-            for t0, t1 in ((0, VCOLS), (VCOLS, T)):
-                nc.vector.quantize_mx(
-                    out=c_a[:, t0:t1].bitcast(FP8X4),
-                    scales=s_a[:, t0:t1],
-                    in_=xb[:, t0:t1, :].rearrange("p t j -> p (t j)"),
-                )
+            xb.append(xb_a)
             codes.append(c_a)
             scales.append(s_a)
+
+        def interleave(copy, a, t0, t1):
+            for p0, p1, piece in raw[a]:
+                if p0 <= t0 and t1 <= p1:
+                    copy(xb[a][:, t0:t1, :], piece[:, :, t0 - p0 : t1 - p0].rearrange("p j t -> p t j"))
+
+        def quantize(a, t0, t1):
+            nc.vector.quantize_mx(
+                out=codes[a][:, t0:t1].bitcast(FP8X4),
+                scales=scales[a][:, t0:t1],
+                in_=xb[a][:, t0:t1, :].rearrange("p t j -> p (t j)"),
+            )
 
         def xr_pass(a, t, h):
             rhs, rhs_scale = w_operand(a, h)
@@ -137,12 +143,31 @@ def tile_mix_xres_tm_mul_kernel(tc, x4_words, x4_scales, xr, w4_words, w4_scales
                 lhsT_scale=scales[a][:, P * t : P * (t + 1)],
                 rhs=rhs,
                 rhs_scale=rhs_scale,
-                start=False,
+                start=(a == 0 and t < FIRST),
                 stop=(a == A - 1),
             )
 
-        for a, tiles in ((0, TT), (1, EARLY)):
-            for t in range(tiles):
+        for t, copy in enumerate((nc.vector.tensor_copy, nc.scalar.copy)):
+            interleave(copy, 0, P * t, P * (t + 1))
+            quantize(0, P * t, P * (t + 1))
+            for h in range(NH):
+                xr_pass(0, t, h)
+
+        for a in range(A):
+            for h in range(NH):
+                for t in range(TT):
+                    x4_pass(a, t, h)
+
+        for a in range(A):
+            if a > 0:
+                interleave(nc.vector.tensor_copy, a, 0, VCOLS)
+            interleave(nc.scalar.copy, a, VCOLS, T)
+            if a > 0:
+                quantize(a, 0, VCOLS)
+            quantize(a, VCOLS, T)
+
+        for a, tiles in ((0, range(FIRST, TT)), (1, range(EARLY))):
+            for t in tiles:
                 for h in range(NH):
                     xr_pass(a, t, h)
 
@@ -152,11 +177,17 @@ def tile_mix_xres_tm_mul_kernel(tc, x4_words, x4_scales, xr, w4_words, w4_scales
             for h in range(NH):
                 for a in range(2 if t < EARLY else 1, A):
                     xr_pass(a, t, h)
-                cols = slice(HALF * h, HALF * (h + 1))
-                nc.vector.tensor_tensor(
-                    out=result[:, cols], in0=banks[NH * t + h][:], in1=g_sb[t][:, cols], op=mybir.AluOpType.mult
-                )
-                if t == TT - 1:
-                    nc.sync.dma_start(out=out[rows, cols], in_=result[:, cols])
+                parts = 2 if (t, h) == (TT - 1, NH - 1) else 1
+                for j in range(parts):
+                    b_cols = slice(HALF // parts * j, HALF // parts * (j + 1))
+                    cols = slice(HALF * h + b_cols.start, HALF * h + b_cols.stop)
+                    nc.vector.tensor_tensor(
+                        out=result[:, cols],
+                        in0=banks[NH * t + h][:, b_cols],
+                        in1=g_sb[t][:, cols],
+                        op=mybir.AluOpType.mult,
+                    )
+                    if t == TT - 1:
+                        nc.sync.dma_start(out=out[rows, cols], in_=result[:, cols])
             if t < TT - 1:
                 nc.sync.dma_start(out=out[rows, :], in_=result[:])

from contextlib import ExitStack

import concourse.mybir as mybir

K, N, T = 2048, 1024, 512
FLOPS = 2 * 2 * K * N * T

F32 = mybir.dt.float32
BF16 = mybir.dt.bfloat16
U32 = mybir.dt.uint32
I32 = mybir.dt.int32
U8 = mybir.dt.uint8
FP8X4 = mybir.dt.float8_e4m3fn_x4
FP4X4 = mybir.dt.float4_e2m1fn_x4

P = 128
A = K // 512
TT = T // P
NH = 2
HALF = N // NH
VCOLS = 256
FIRST = 2
EARLY = 2


def tile_mix_xres_tm_mul_kernel(tc, x4_words, x4_scales, xr, w4_words, w4_scales, g, out):
    nc = tc.nc
    with ExitStack() as ctx:
        keep = ctx.enter_context(tc.tile_pool(name="keep", bufs=1))
        psum = ctx.enter_context(tc.psum_pool(name="psum", bufs=1))
        ctx.enter_context(tc.manual_schedule())

        x0 = keep.tile([P, 1, 2 * T], U8, name="x0", align_bytes=256)
        x123 = keep.tile([P, A - 1, 2 * T], U8, name="x123", align_bytes=256)
        w0 = keep.tile([P, 1, 2 * N], U8, name="w0", align_bytes=256)
        w1 = keep.tile([P, 1, 2 * N], U8, name="w1", align_bytes=256)
        w23 = keep.tile([P, 2, 2 * N], U8, name="w23", align_bytes=256)
        xs = keep.tile([P, A, T], U8, name="xs", align_bytes=256)
        ws = keep.tile([P, A, N], U8, name="ws", align_bytes=256)
        dummy = keep.tile([P, 8], F32, name="dummy")
        dummy_out = keep.tile([P, 8], F32, name="dummy_out")

        def flat_i32(t):
            return t[:].rearrange("p a n -> p (a n)").bitcast(I32)

        nc.vector.memset(flat_i32(ws), 0)
        nc.vector.memset(flat_i32(xs), 0)
        nc.vector.memset(dummy[:], 0.0)

        def load_scales(engine, tile, dram, r):
            n4 = dram.shape[2] // 4
            engine.dma_start(
                out=flat_i32(tile)[r:P:32, :].rearrange("q (a n) -> q a n", n=n4),
                in_=dram.bitcast(I32)[:, r:16:4, :].rearrange("a q n -> q a n"),
            )

        raw = []
        for a, widths in enumerate(((VCOLS, T - VCOLS), (T,), (T,), (T,))):
            pieces, t0 = [], 0
            for width in widths:
                piece = keep.tile([P, 4, width], F32, name="raw%d_%d" % (a, t0), align_bytes=256)
                pieces.append((t0, t0 + width, piece))
                t0 += width
            raw.append(pieces)

        def load_raw(a, i):
            t0, t1, piece = raw[a][i]
            nc.sync.dma_start(
                out=piece[:], in_=xr[512 * a : 512 * (a + 1), t0:t1].rearrange("(p j) t -> p j t", j=4)
            )

        load_raw(0, 0)
        nc.sync.dma_start(out=w0[:, 0, :], in_=w4_words[0])
        for r in range(4):
            load_scales(nc.sync, ws, w4_scales, r)
        nc.sync.dma_start(out=x0[:, 0, :], in_=x4_words[0])
        for r in range(4):
            load_scales(nc.sync, xs, x4_scales, r)
        nc.sync.dma_start(out=w1[:, 0, :], in_=w4_words[1])
        nc.sync.dma_start(out=x123[:], in_=x4_words[1:A].rearrange("a p n -> p a n"))
        nc.sync.dma_start(out=w23[:], in_=w4_words[2:A].rearrange("a p n -> p a n"))
        nc.scalar.copy(dummy_out[:], dummy[:])
        load_raw(0, 1)
        for a in range(1, A):
            load_raw(a, 0)
        g_sb = []
        for t in range(TT):
            g_t = keep.tile([P, N], F32, name="g%d" % t, align_bytes=256)
            nc.sync.dma_start(out=g_t[:], in_=g[P * t : P * (t + 1), :])
            g_sb.append(g_t)

        banks = []
        for i in range(TT * NH):
            bank = psum.tile([P, HALF], F32, name="bank%d" % i)
            banks.append(bank)

        def w_operand(a, h):
            words, b = ((w0, 0), (w1, 0), (w23, 0), (w23, 1))[a]
            return (
                words[:, b, 2 * HALF * h : 2 * HALF * (h + 1)].bitcast(FP4X4),
                ws[:, a, HALF * h : HALF * (h + 1)],
            )

        def x4_pass(a, t, h):
            words, b = (x0, 0) if a == 0 else (x123, a - 1)
            rhs, rhs_scale = w_operand(a, h)
            nc.tensor.matmul_mx(
                out=banks[NH * t + h][:],
                lhsT=words[:, b, 2 * P * t : 2 * P * (t + 1)].bitcast(FP4X4),
                lhsT_scale=xs[:, a, P * t : P * (t + 1)],
                rhs=rhs,
                rhs_scale=rhs_scale,
                start=(a == 0 and t >= FIRST),
                stop=False,
            )

        xb, codes, scales = [], [], []
        for a in range(A):
            xb_a = keep.tile([P, T, 4], BF16, name="xb%d" % a, align_bytes=256)
            c_a = keep.tile([P, T], U32, name="codes%d" % a, align_bytes=256)
            s_a = keep.tile([P, T], U8, name="scales%d" % a, align_bytes=256)
            xb.append(xb_a)
            codes.append(c_a)
            scales.append(s_a)

        def interleave(copy, a, t0, t1):
            for p0, p1, piece in raw[a]:
                if p0 <= t0 and t1 <= p1:
                    copy(xb[a][:, t0:t1, :], piece[:, :, t0 - p0 : t1 - p0].rearrange("p j t -> p t j"))

        def quantize(a, t0, t1):
            nc.vector.quantize_mx(
                out=codes[a][:, t0:t1].bitcast(FP8X4),
                scales=scales[a][:, t0:t1],
                in_=xb[a][:, t0:t1, :].rearrange("p t j -> p (t j)"),
            )

        def xr_pass(a, t, h):
            rhs, rhs_scale = w_operand(a, h)
            nc.tensor.matmul_mx(
                out=banks[NH * t + h][:],
                lhsT=codes[a][:, P * t : P * (t + 1)].bitcast(FP8X4),
                lhsT_scale=scales[a][:, P * t : P * (t + 1)],
                rhs=rhs,
                rhs_scale=rhs_scale,
                start=(a == 0 and t < FIRST),
                stop=(a == A - 1),
            )

        for t, copy in enumerate((nc.vector.tensor_copy, nc.scalar.copy)):
            interleave(copy, 0, P * t, P * (t + 1))
            quantize(0, P * t, P * (t + 1))
            for h in range(NH):
                xr_pass(0, t, h)

        for a in range(A):
            for h in range(NH):
                for t in range(TT):
                    x4_pass(a, t, h)

        for a in range(A):
            if a > 0:
                interleave(nc.vector.tensor_copy, a, 0, VCOLS)
            interleave(nc.scalar.copy, a, VCOLS, T)
            if a > 0:
                quantize(a, 0, VCOLS)
            quantize(a, VCOLS, T)

        for a, tiles in ((0, range(FIRST, TT)), (1, range(EARLY))):
            for t in tiles:
                for h in range(NH):
                    xr_pass(a, t, h)

        for t in range(TT):
            result = keep.tile([P, N], F32, name="result%d" % t, align_bytes=256)
            rows = slice(P * t, P * (t + 1))
            for h in range(NH):
                for a in range(2 if t < EARLY else 1, A):
                    xr_pass(a, t, h)
                parts = 2 if (t, h) == (TT - 1, NH - 1) else 1
                for j in range(parts):
                    b_cols = slice(HALF // parts * j, HALF // parts * (j + 1))
                    cols = slice(HALF * h + b_cols.start, HALF * h + b_cols.stop)
                    nc.vector.tensor_tensor(
                        out=result[:, cols],
                        in0=banks[NH * t + h][:, b_cols],
                        in1=g_sb[t][:, cols],
                        op=mybir.AluOpType.mult,
                    )
                    if t == TT - 1:
                        nc.sync.dma_start(out=out[rows, cols], in_=result[:, cols])
            if t < TT - 1:
                nc.sync.dma_start(out=out[rows, :], in_=result[:])
